import numpy as np
import ml_dtypes


def mxq(x, axis, fmt="e4m3"):
    dtype, down = {"e4m3": (ml_dtypes.float8_e4m3fn, 7), "e5m2": (ml_dtypes.float8_e5m2, 14)}[fmt]
    v = np.moveaxis(np.asarray(x, np.float32).astype(ml_dtypes.bfloat16).astype(np.float64), axis, -1)
    blocks = v.reshape(v.shape[:-1] + (-1, 32))
    amax = np.abs(blocks).max(-1, keepdims=True)
    byte = np.maximum(np.where(amax > 0, np.frexp(amax)[1] - 1 + 127, 0) - down, 1)
    scale = np.exp2(byte - 127.0)
    codes = (blocks / scale).astype(np.float32).astype(dtype).astype(np.float64)
    return np.moveaxis((codes * scale).reshape(v.shape), -1, axis)


WIDE = False


def mx_kscale(k):
    if not WIDE:
        return np.ones(k)
    levels = np.array([10, -10, 5, -5, 0])
    if k % 512:
        return np.exp2(np.random.permutation(np.resize(levels, k // 32))).repeat(32)
    a = np.empty((k // 512, 16))
    for p in range(k // 512):
        a[p, :8] = np.random.permutation(np.resize(levels, 8))
        for g in range(8):
            far = levels[np.abs(levels - a[p, g]) >= 10]
            a[p, g + 8] = far[np.random.randint(len(far))]
    return np.exp2(a.ravel()).repeat(32)


def f64(x):
    return np.asarray(x).astype(np.float64)


def striped(idx):
    return np.tile(idx.reshape(-1, 16).T, (8, 1)).astype(np.uint16)


def unstriped(offs):
    return offs[:16].T.reshape(-1).astype(np.int64)


def striped8(idx):
    return np.concatenate([x.reshape(-1, 16).T for x in idx]).astype(np.uint16)


def runs(offs, k):
    lists = np.stack([offs[16 * r : 16 * r + 16].T.reshape(-1) for r in range(8)]).astype(np.int64)
    return lists[np.arange(k) % 512 // 64]


def pack_weight(w):
    k, n = w.shape
    w = f64(np.asarray(w, np.float32).astype(ml_dtypes.bfloat16)).reshape(k // 32, 32, n)
    amax = np.abs(w).max(1)
    byte = np.clip(np.where(amax > 0, np.frexp(amax)[1] - 1 + 127 - 7, 1), 1, 254)
    scaled = (w * np.exp2(127.0 - byte)[:, None, :]).reshape(k, n).astype(np.float32)
    words = np.ascontiguousarray(scaled.reshape(k // 512, 128, 4, n).transpose(0, 1, 3, 2)).astype(ml_dtypes.float8_e4m3fn).view(np.uint8)
    return words, np.ascontiguousarray(byte.astype(np.uint8).reshape(k // 512, 16, n))


def unpack_weight(words, scales):
    g, p, n, _ = words.shape
    vals = np.ascontiguousarray(words).view(ml_dtypes.float8_e4m3fn).astype(np.float64) * np.repeat(np.exp2(scales.astype(np.float64) - 127.0), 8, axis=1)[..., None]
    return vals.transpose(0, 1, 3, 2).reshape(g * 512, n)


K, T, S, N, G, H, W = 512, 1024, 256, 512, 2048, 512, 128


def setup_inputs():
    n = np.random.standard_normal
    s = mx_kscale(K)[:, None]
    u = mx_kscale(K)
    packed_xT = pack_weight(n((K, T)) * s)
    packed_dT = pack_weight(n((K, G)) / s)
    packed_w1 = pack_weight(n((H, N)) / np.sqrt(2 * H) / u[:, None])
    packed_w2 = pack_weight(n((K, N)) / np.sqrt(2 * K) / s)
    perm = np.random.permutation(S)
    perm2 = np.random.permutation(S)
    perm3 = np.random.permutation(S)
    return {
        "x_words": packed_xT[0],
        "x_scales": packed_xT[1],
        "d_words": packed_dT[0],
        "d_scales": packed_dT[1],
        "gn": (np.random.uniform(0.5, 1.5, (H, 1)) * u[:, None]).astype(np.float32),
        "w1_words": packed_w1[0],
        "w1_scales": packed_w1[1],
        "w2_words": packed_w2[0],
        "w2_scales": packed_w2[1],
        "offs": striped(np.random.permutation(T)[:S]),
        "k1": striped8(np.random.randint(0, G, (8, H))),
        "two": striped(np.random.permutation(T)[:S]),
        "k2": striped8(np.random.randint(0, G, (8, H))),
        "hz": striped8(np.random.randint(0, T, (8, S))),
        "k3": striped8(np.random.randint(0, G, (8, H))),
        "n1": striped(perm[:W]),
        "n2": striped(perm[W:]),
        "n3": striped(perm2[:W]),
        "n4": striped(perm2[W:]),
        "n5": striped(np.random.permutation(S)),
        "duo": striped(np.random.permutation(T)[:S]),
        "n6": striped(perm3[:W]),
        "n7": striped(perm3[W:]),
    }


def reference(x_words, x_scales, d_words, d_scales, gn, w1_words, w1_scales, w2_words, w2_scales, offs, k1, two, k2, hz, k3, n1, n2, n3, n4, n5, duo, n6, n7):
    d_k1 = unpack_weight(d_words, d_scales)[np.arange(K)[:, None], runs(k1, K)]
    xq = unpack_weight(x_words, x_scales)[:, unstriped(offs)]
    d_k2 = unpack_weight(d_words, d_scales)[np.arange(K)[:, None], runs(k2, K)]
    x_two = unpack_weight(x_words, x_scales)[:, unstriped(two)]
    d_k3 = unpack_weight(d_words, d_scales)[np.arange(K)[:, None], runs(k3, K)]
    x_hz = unpack_weight(x_words, x_scales)[np.arange(K)[:, None], runs(hz, K)]
    h = 0.0625 * (d_k1.T @ xq + d_k2.T @ x_two + d_k3.T @ x_hz)
    pa = h[:, unstriped(n1)]
    pb = h[:, unstriped(n2)]
    rb = pa + pb
    ra = np.minimum(pa, pb)
    ua = np.zeros((H, S))
    ua[:, unstriped(n3)] = ra
    ub = ua.copy()
    ub[:, unstriped(n4)] = rb
    ds = np.zeros((H, S))
    ds[:, unstriped(n5)] = ub
    z = f64(gn) * (ub - ds)
    x_duo = unpack_weight(x_words, x_scales)[:, unstriped(duo)]
    h2 = unpack_weight(w1_words, w1_scales).T @ mxq(z, 0, "e4m3") + unpack_weight(w2_words, w2_scales).T @ x_duo
    pb2 = h2[:, unstriped(n7)]
    pa2 = h2[:, unstriped(n6)]
    rb2 = pb2 - (0.5 * pa2)
    ra2 = np.sqrt((pa2) ** 2 + (pb2) ** 2 + 0.25)
    ua2 = np.zeros((N, S))
    ua2[:, unstriped(n6)] = ra2
    out = ua2.copy()
    out[:, unstriped(n7)] = rb2
    return out

@@ -1,0 +1,275 @@
+from contextlib import ExitStack
+
+import concourse.mybir as mybir
+
+K, T, S, N, G, H, W = 512, 1024, 256, 512, 2048, 512, 128
+FLOPS = 2 * K * S * (3 * H + 2 * N)
+
+F32 = mybir.dt.float32
+BF16 = mybir.dt.bfloat16
+I32 = mybir.dt.int32
+U32 = mybir.dt.uint32
+U16 = mybir.dt.uint16
+U8 = mybir.dt.uint8
+FP8X4 = mybir.dt.float8_e4m3fn_x4
+ALU = mybir.AluOpType
+ACT = mybir.ActivationFunctionType
+
+P = 128
+HALF = P // 2
+PACK = 4
+CODED = 3
+PIECE = H // 2
+
+
+def tile_picked_mtthzntcpsdpolar_none_p_kernel(
+    tc, x_words, x_scales, d_words, d_scales, gn, w1_words, w1_scales, w2_words, w2_scales,
+    offs, k1, two, k2, hz, k3, n1, n2, n3, n4, n5, duo, n6, n7, out,
+):
+    nc = tc.nc
+    with ExitStack() as ctx:
+        held = ctx.enter_context(tc.tile_pool(name="held", bufs=1))
+        psum = ctx.enter_context(tc.psum_pool(name="psum", bufs=1))
+
+        def sbuf(name, shape, dtype, tag=None):
+            return held.tile(shape, dtype, name=name, tag=tag or name, align_bytes=64)
+
+        def load_list(name, src):
+            lst = held.tile(list(src.shape), U16, name=name)
+            nc.sync.dma_start(lst[:], src)
+            return lst
+
+        def load_words(name, src, queue):
+            words = sbuf(name, [P, src.shape[2]], U32)
+            queue.dma_start(words[:].bitcast(I32), src[0].rearrange("p n t -> p (n t)").bitcast(I32))
+            return words
+
+        x_bytes = sbuf("x_bytes", [P, T], U8)
+        d_bytes = sbuf("d_bytes", [P, G], U8)
+        w_bytes = sbuf("w_bytes", [P, 2 * N], U8)
+        moved0 = sbuf("moved0", [P, CODED * (S + PIECE)], U8)
+        moved1 = sbuf("moved1", [P, CODED * PIECE], U8)
+        duop = sbuf("duop", [P, S], U8)
+        for plane in (x_bytes, d_bytes, moved0, moved1, duop, w_bytes):
+            nc.gpsimd.memset(plane[:].bitcast(I32), 0)
+        nc.scalar.dma_start(x_bytes[0:P:8, :].bitcast(I32), x_scales[0].bitcast(I32))
+        nc.scalar.dma_start(d_bytes[0:P:8, :].bitcast(I32), d_scales[0].bitcast(I32))
+        l_offs = load_list("l_offs", offs)
+        l_two = load_list("l_two", two)
+        xw = load_words("xw", x_words, nc.sync)
+        l_hz = load_list("l_hz", hz)
+        dw = load_words("dw", d_words, nc.sync)
+        l_k = [load_list("l_k1", k1), load_list("l_k2", k2), load_list("l_k3", k3)]
+        l_n1 = load_list("l_n1", n1)
+        l_n2 = load_list("l_n2", n2)
+        l_n3 = load_list("l_n3", n3)
+        l_n4 = load_list("l_n4", n4)
+        l_n5 = load_list("l_n5", n5)
+        l_duo = load_list("l_duo", duo)
+        l_n6 = load_list("l_n6", n6)
+        l_n7 = load_list("l_n7", n7)
+        w2w = load_words("w2w", w2_words, nc.sync)
+        w1w = load_words("w1w", w1_words, nc.sync)
+        gain = sbuf("gain", [P, PACK], F32)
+        nc.gpsimd.dma_start(gain[:], gn.rearrange("(p t) o -> p (t o)", t=PACK))
+        for j, src in enumerate((w1_scales, w2_scales)):
+            for q in range(4):
+                nc.gpsimd.dma_start(
+                    w_bytes[32 * q : 32 * q + 4, j * N : (j + 1) * N].bitcast(I32),
+                    src[0][4 * q : 4 * q + 4, :].bitcast(I32),
+                )
+        l_x = [l_offs, l_two, l_hz]
+
+        def gather_tokens(got, table, lists):
+            for j, lst in enumerate(lists):
+                nc.vector.tensor_copy(got[:, j * S : (j + 1) * S], table[:].indirect(lst[:]))
+
+        def gather_codes(got, table, piece):
+            cols = slice(piece * PIECE // 16, (piece + 1) * PIECE // 16)
+            for j in range(CODED):
+                nc.vector.tensor_copy(got[:, j * PIECE : (j + 1) * PIECE], table[:].indirect(l_k[j][:, cols]))
+
+        def deal_low(dst, got):
+            nc.vector.tensor_copy(
+                dst.rearrange("p (l t m) -> p l m t", l=CODED, t=2),
+                got.rearrange("p (l m t) -> p l m t", l=CODED, t=PACK)[:, :, :, 0:2],
+            )
+
+        def deal_high(dst, got, piece):
+            nc.vector.tensor_copy(
+                dst.rearrange("p (t l h m) -> p h l m t", t=2, l=CODED, h=2)[:, piece],
+                got.rearrange("p (l m t) -> p l m t", l=CODED, t=PACK)[:, :, :, 2:4],
+            )
+
+        def move_rows(dst, src, queues):
+            for q in range(4):
+                queues[q % len(queues)].dma_start(
+                    dst[32 * q : 32 * q + 4, :].bitcast(I32), src[32 * q : 32 * q + 32 : 8, :].bitcast(I32)
+                )
+
+        XS = CODED * S
+        CT = CODED * P
+
+        bytes0 = sbuf("bytes0", [P, XS + CODED * PIECE], U8, "bytes")
+        gather_tokens(bytes0[:, :XS], x_bytes, l_x)
+        gather_codes(bytes0[:, XS:], d_bytes, 0)
+        move_rows(moved0, bytes0, (nc.scalar, nc.sync))
+        xg = sbuf("xg", [P, XS], U32)
+        gather_tokens(xg[:], xw, l_x)
+        dg0 = sbuf("dg0", [P, CODED * PIECE], U32)
+        gather_codes(dg0[:], dw, 0)
+        codes0 = sbuf("codes0", [P, CT], U32)
+        deal_low(codes0[:], dg0[:])
+        plane0 = sbuf("plane0", [P, CT], U8)
+        deal_low(plane0[:], moved0[:, XS:])
+
+        def product_h(name, codes, plane):
+            acc = psum.tile([P, S], F32, name=name)
+            for j in range(CODED):
+                nc.tensor.matmul_mx(
+                    out=acc[:],
+                    lhsT=codes[:, j * P : (j + 1) * P].bitcast(FP8X4),
+                    lhsT_scale=plane[:, j * P : (j + 1) * P],
+                    rhs=xg[:, j * S : (j + 1) * S].bitcast(FP8X4),
+                    rhs_scale=moved0[:, j * S : (j + 1) * S],
+                    start=(j == 0),
+                    stop=(j == CODED - 1),
+                )
+            return acc
+
+        h = [sbuf("h%d" % x, [P, S], F32) for x in range(4)]
+        ub = [sbuf("ub%d" % x, [P, S], F32) for x in range(4)]
+        ds = [sbuf("ds%d" % x, [P, 2 * S], F32) for x in range(4)]
+        res = {}
+
+        def fetch1(x, tag):
+            pair = sbuf("pair%d" % x, [P, S], F32, tag)
+            res[x] = sbuf("res%d" % x, [P, S], F32)
+            nc.scalar.activation(pair[:, :W], h[x][:].indirect(l_n1[:]), ACT.Copy)
+            nc.scalar.activation(pair[:, W:], h[x][:].indirect(l_n2[:]), ACT.Copy)
+            nc.vector.tensor_tensor(res[x][:, :W], pair[:, :W], pair[:, W:], ALU.min)
+            nc.vector.tensor_tensor(res[x][:, W:], pair[:, :W], pair[:, W:], ALU.add)
+
+        def put1(x):
+            nc.scalar.activation(ub[x][:].indirect(l_n3[:]), res[x][:, :W], ACT.Copy)
+            nc.scalar.activation(ub[x][:].indirect(l_n4[:]), res[x][:, W:], ACT.Copy)
+
+        def send1(x):
+            nc.scalar.activation(ds[x][:].indirect(l_n5[:]), ub[x][:], ACT.Copy)
+
+        acc0 = product_h("acc0", codes0[:], plane0[:])
+        nc.scalar.activation(h[0][:], acc0[:], ACT.Copy, scale=0.0625)
+        fetch1(0, "pair0")
+        put1(0)
+        send1(0)
+
+        bytes1 = sbuf("bytes1", [P, CODED * PIECE], U8, "bytes")
+        gather_codes(bytes1[:], d_bytes, 1)
+        move_rows(moved1, bytes1, (nc.sync,))
+        dg1 = sbuf("dg1", [P, CODED * PIECE], U32, "pair0")
+        gather_codes(dg1[:], dw, 1)
+        codes1 = sbuf("codes1", [P, CT], U32)
+        deal_low(codes1[:], dg1[:])
+        plane1 = sbuf("plane1", [P, CT], U8)
+        deal_low(plane1[:], moved1[:])
+        acc1 = product_h("acc1", codes1[:], plane1[:])
+        nc.vector.tensor_scalar(h[1][:], acc1[:], 0.0625, None, ALU.mult)
+        fetch1(1, "pair1")
+        codes23 = sbuf("codes23", [P, 2 * CT], U32, "codes1")
+        plane23 = sbuf("plane23", [P, 2 * CT], U8, "plane1")
+        deal_high(codes23[:], dg0[:], 0)
+        deal_high(codes23[:], dg1[:], 1)
+        deal_high(plane23[:], moved0[:, XS:], 0)
+        deal_high(plane23[:], moved1[:], 1)
+        for x in (2, 3):
+            cols = slice((x - 2) * CT, (x - 1) * CT)
+            acc = product_h("acc%d" % x, codes23[:, cols], plane23[:, cols])
+            nc.vector.tensor_scalar(h[x][:], acc[:], 0.0625, None, ALU.mult)
+        put1(1)
+        fetch1(2, "res1")
+        send1(1)
+
+        slot0 = sbuf("slot0", [P, S], F32)
+        slot1 = sbuf("slot1", [P, S], F32)
+        low1 = sbuf("low1", [P, S], F32)
+        zi = sbuf("zi", [P, S, PACK], BF16)
+        nc.vector.tensor_tensor(slot0[:], ub[0][:], ds[0][:, :S], ALU.subtract)
+        nc.sync.dma_start(slot1[:HALF, :], slot0[HALF:, :])
+
+        duob = sbuf("duob", [P, S], U8, "res1")
+        gather_tokens(duob[:], x_bytes, [l_duo])
+        move_rows(duop, duob, (nc.sync,))
+        duog = sbuf("duog", [P, S], U32, "h2")
+        gather_tokens(duog[:], xw, [l_duo])
+        acc2 = [psum.tile([P, S], F32, name="out_acc%d" % t) for t in range(4)]
+        for t in range(4):
+            nc.tensor.matmul_mx(
+                out=acc2[t][:],
+                lhsT=w2w[:, t * P : (t + 1) * P].bitcast(FP8X4),
+                lhsT_scale=w_bytes[:, N + t * P : N + (t + 1) * P],
+                rhs=duog[:].bitcast(FP8X4),
+                rhs_scale=duop[:],
+                start=True,
+                stop=False,
+            )
+        loss = sbuf("loss", [P, PACK], F32)
+        nc.gpsimd.tensor_scalar(loss[:], gain[:], -1.0, None, ALU.mult)
+
+        put1(2)
+        fetch1(3, "res2")
+        send1(2)
+        nc.vector.tensor_tensor(low1[:HALF, :], ub[1][:HALF, :], ds[1][:HALF, :S], ALU.subtract)
+        nc.sync.dma_start(slot0[HALF:, :], low1[:HALF, :])
+        nc.vector.tensor_tensor(slot1[HALF:, :], ub[1][HALF:, :], ds[1][HALF:, :S], ALU.subtract)
+        put1(3)
+        send1(3)
+        nc.vector.tensor_scalar(zi[:, :, 0], slot0[:], gain[:, 0:1], None, ALU.mult)
+        nc.vector.tensor_scalar(zi[:, :, 1], slot1[:], gain[:, 1:2], None, ALU.mult)
+        for x in (2, 3):
+            scaled = sbuf("scaled%d" % x, [P, S], F32)
+            nc.vector.tensor_scalar(scaled[:], ub[x][:], gain[:, x : x + 1], None, ALU.mult)
+            nc.vector.scalar_tensor_tensor(zi[:, :, x], ds[x][:, :S], loss[:, x : x + 1], scaled[:], ALU.mult, ALU.add)
+
+        zq = sbuf("zq", [P, S], U32)
+        zs = sbuf("zs", [P, S], U8)
+        nc.vector.quantize_mx(out=zq[:].bitcast(FP8X4), scales=zs[:], in_=zi[:].rearrange("p c t -> p (c t)"))
+        for t in range(4):
+            nc.tensor.matmul_mx(
+                out=acc2[t][:],
+                lhsT=w1w[:, t * P : (t + 1) * P].bitcast(FP8X4),
+                lhsT_scale=w_bytes[:, t * P : (t + 1) * P],
+                rhs=zq[:].bitcast(FP8X4),
+                rhs_scale=zs[:],
+                start=False,
+                stop=True,
+            )
+
+        h2 = [sbuf("g%d" % t, [P, S], F32) for t in range(4)]
+        pair2 = [sbuf("pairb%d" % t, [P, S], F32) for t in range(4)]
+        square = [sbuf("square%d" % t, [P, S], F32) for t in range(4)]
+        diff2 = [sbuf("diffb%d" % t, [P, W], F32) for t in range(4)]
+        radic = [sbuf("radic%d" % t, [P, W], F32) for t in range(4)]
+        root = [sbuf("root%d" % t, [P, W], F32) for t in range(4)]
+        done = [sbuf("done%d" % t, [P, S], F32) for t in range(4)]
+
+        def fetch2(t):
+            nc.scalar.activation(pair2[t][:, :W], h2[t][:].indirect(l_n6[:]), ACT.Copy)
+            nc.scalar.activation(pair2[t][:, W:], h2[t][:].indirect(l_n7[:]), ACT.Copy)
+            nc.vector.scalar_tensor_tensor(diff2[t][:], pair2[t][:, :W], -0.5, pair2[t][:, W:], ALU.mult, ALU.add)
+            nc.vector.tensor_tensor(square[t][:], pair2[t][:], pair2[t][:], ALU.mult)
+            nc.vector.scalar_tensor_tensor(radic[t][:], square[t][:, :W], 0.25, square[t][:, W:], ALU.add, ALU.add)
+
+        def put2(t):
+            nc.scalar.activation(done[t][:].indirect(l_n7[:]), diff2[t][:], ACT.Copy)
+            nc.scalar.activation(root[t][:], radic[t][:], ACT.Sqrt)
+            nc.scalar.activation(done[t][:].indirect(l_n6[:]), root[t][:], ACT.Copy)
+            nc.sync.dma_start(out[t * P : (t + 1) * P, :], done[t][:])
+
+        nc.scalar.activation(h2[0][:], acc2[0][:], ACT.Copy)
+        for t in range(1, 4):
+            nc.vector.tensor_copy(h2[t][:], acc2[t][:])
+        fetch2(0)
+        for t in range(4):
+            if t + 1 < 4:
+                fetch2(t + 1)
+            put2(t)

@@ -50,16 +50,18 @@ def tile_picked_mtthzntcpsdpolar_none_p_kernel(
         moved0 = sbuf("moved0", [P, CODED * (S + PIECE)], U8)
         moved1 = sbuf("moved1", [P, CODED * PIECE], U8)
         duop = sbuf("duop", [P, S], U8)
-        for plane in (x_bytes, d_bytes, moved0, moved1, duop, w_bytes):
+        for plane in (d_bytes, moved0):
+            nc.vector.memset(plane[:].bitcast(I32), 0)
+        for plane in (x_bytes, moved1, duop, w_bytes):
             nc.gpsimd.memset(plane[:].bitcast(I32), 0)
-        nc.scalar.dma_start(x_bytes[0:P:8, :].bitcast(I32), x_scales[0].bitcast(I32))
-        nc.scalar.dma_start(d_bytes[0:P:8, :].bitcast(I32), d_scales[0].bitcast(I32))
+        nc.sync.dma_start(x_bytes[0:P:8, :].bitcast(I32), x_scales[0].bitcast(I32))
+        nc.sync.dma_start(d_bytes[0:P:8, :].bitcast(I32), d_scales[0].bitcast(I32))
         l_offs = load_list("l_offs", offs)
         l_two = load_list("l_two", two)
-        xw = load_words("xw", x_words, nc.sync)
         l_hz = load_list("l_hz", hz)
-        dw = load_words("dw", d_words, nc.sync)
         l_k = [load_list("l_k1", k1), load_list("l_k2", k2), load_list("l_k3", k3)]
+        xw = load_words("xw", x_words, nc.sync)
+        dw = load_words("dw", d_words, nc.sync)
         l_n1 = load_list("l_n1", n1)
         l_n2 = load_list("l_n2", n2)
         l_n3 = load_list("l_n3", n3)
@@ -71,7 +73,8 @@ def tile_picked_mtthzntcpsdpolar_none_p_kernel(
         w2w = load_words("w2w", w2_words, nc.sync)
         w1w = load_words("w1w", w1_words, nc.sync)
         gain = sbuf("gain", [P, PACK], F32)
-        nc.gpsimd.dma_start(gain[:], gn.rearrange("(p t) o -> p (t o)", t=PACK))
+        with nc.allow_non_contiguous_dma(reason="one gain a row"):
+            nc.gpsimd.dma_start(gain[:], gn.rearrange("(t p) o -> p (t o)", p=P))
         for j, src in enumerate((w1_scales, w2_scales)):
             for q in range(4):
                 nc.gpsimd.dma_start(
@@ -84,22 +87,10 @@ def tile_picked_mtthzntcpsdpolar_none_p_kernel(
             for j, lst in enumerate(lists):
                 nc.vector.tensor_copy(got[:, j * S : (j + 1) * S], table[:].indirect(lst[:]))
 
-        def gather_codes(got, table, piece):
+        def gather_codes(got, table, piece, lists):
             cols = slice(piece * PIECE // 16, (piece + 1) * PIECE // 16)
-            for j in range(CODED):
-                nc.vector.tensor_copy(got[:, j * PIECE : (j + 1) * PIECE], table[:].indirect(l_k[j][:, cols]))
-
-        def deal_low(dst, got):
-            nc.vector.tensor_copy(
-                dst.rearrange("p (l t m) -> p l m t", l=CODED, t=2),
-                got.rearrange("p (l m t) -> p l m t", l=CODED, t=PACK)[:, :, :, 0:2],
-            )
-
-        def deal_high(dst, got, piece):
-            nc.vector.tensor_copy(
-                dst.rearrange("p (t l h m) -> p h l m t", t=2, l=CODED, h=2)[:, piece],
-                got.rearrange("p (l m t) -> p l m t", l=CODED, t=PACK)[:, :, :, 2:4],
-            )
+            for j, lst in enumerate(lists):
+                nc.vector.tensor_copy(got[:, j * PIECE : (j + 1) * PIECE], table[:].indirect(lst[:, cols]))
 
         def move_rows(dst, src, queues):
             for q in range(4):
@@ -112,91 +103,90 @@ def tile_picked_mtthzntcpsdpolar_none_p_kernel(
 
         bytes0 = sbuf("bytes0", [P, XS + CODED * PIECE], U8, "bytes")
         gather_tokens(bytes0[:, :XS], x_bytes, l_x)
-        gather_codes(bytes0[:, XS:], d_bytes, 0)
-        move_rows(moved0, bytes0, (nc.scalar, nc.sync))
+        gather_codes(bytes0[:, XS:], d_bytes, 0, l_k)
+        move_rows(moved0, bytes0, (nc.scalar,))
         xg = sbuf("xg", [P, XS], U32)
         gather_tokens(xg[:], xw, l_x)
         dg0 = sbuf("dg0", [P, CODED * PIECE], U32)
-        gather_codes(dg0[:], dw, 0)
-        codes0 = sbuf("codes0", [P, CT], U32)
-        deal_low(codes0[:], dg0[:])
-        plane0 = sbuf("plane0", [P, CT], U8)
-        deal_low(plane0[:], moved0[:, XS:])
+        gather_codes(dg0[:], dw, 0, l_k)
 
-        def product_h(name, codes, plane):
-            acc = psum.tile([P, S], F32, name=name)
+        def product_h(piece, codes, plane):
+            accs = [psum.tile([P, S], F32, name="acc%d" % (2 * piece + u)) for u in range(2)]
             for j in range(CODED):
-                nc.tensor.matmul_mx(
-                    out=acc[:],
-                    lhsT=codes[:, j * P : (j + 1) * P].bitcast(FP8X4),
-                    lhsT_scale=plane[:, j * P : (j + 1) * P],
-                    rhs=xg[:, j * S : (j + 1) * S].bitcast(FP8X4),
-                    rhs_scale=moved0[:, j * S : (j + 1) * S],
-                    start=(j == 0),
-                    stop=(j == CODED - 1),
-                )
-            return acc
+                for u in range(2):
+                    cols = slice(j * PIECE + u * P, j * PIECE + (u + 1) * P)
+                    nc.tensor.matmul_mx(
+                        out=accs[u][:],
+                        lhsT=codes[:, cols].bitcast(FP8X4),
+                        lhsT_scale=plane[:, cols],
+                        rhs=xg[:, j * S : (j + 1) * S].bitcast(FP8X4),
+                        rhs_scale=moved0[:, j * S : (j + 1) * S],
+                        start=(j == 0),
+                        stop=(j == CODED - 1),
+                    )
+            return accs
 
         h = [sbuf("h%d" % x, [P, S], F32) for x in range(4)]
         ub = [sbuf("ub%d" % x, [P, S], F32) for x in range(4)]
         ds = [sbuf("ds%d" % x, [P, 2 * S], F32) for x in range(4)]
-        res = {}
+        res = [sbuf("res%d" % x, [P, S], F32) for x in range(4)]
 
-        def fetch1(x, tag):
-            pair = sbuf("pair%d" % x, [P, S], F32, tag)
-            res[x] = sbuf("res%d" % x, [P, S], F32)
+        def fetch1(x):
+            pair = sbuf("pair%d" % x, [P, S], F32)
             nc.scalar.activation(pair[:, :W], h[x][:].indirect(l_n1[:]), ACT.Copy)
             nc.scalar.activation(pair[:, W:], h[x][:].indirect(l_n2[:]), ACT.Copy)
             nc.vector.tensor_tensor(res[x][:, :W], pair[:, :W], pair[:, W:], ALU.min)
             nc.vector.tensor_tensor(res[x][:, W:], pair[:, :W], pair[:, W:], ALU.add)
 
-        def put1(x):
-            nc.scalar.activation(ub[x][:].indirect(l_n3[:]), res[x][:, :W], ACT.Copy)
-            nc.scalar.activation(ub[x][:].indirect(l_n4[:]), res[x][:, W:], ACT.Copy)
+        def put1(xs):
+            for x in xs:
+                nc.scalar.activation(ub[x][:].indirect(l_n3[:]), res[x][:, :W], ACT.Copy)
+            for x in xs:
+                nc.scalar.activation(ub[x][:].indirect(l_n4[:]), res[x][:, W:], ACT.Copy)
+            for x in xs:
+                nc.scalar.activation(ds[x][:].indirect(l_n5[:]), ub[x][:], ACT.Copy)
 
-        def send1(x):
-            nc.scalar.activation(ds[x][:].indirect(l_n5[:]), ub[x][:], ACT.Copy)
-
-        acc0 = product_h("acc0", codes0[:], plane0[:])
-        nc.scalar.activation(h[0][:], acc0[:], ACT.Copy, scale=0.0625)
-        fetch1(0, "pair0")
-        put1(0)
-        send1(0)
+        accs = product_h(0, dg0[:], moved0[:, XS:])
+        nc.scalar.activation(h[0][:], accs[0][:], ACT.Copy, scale=0.0625)
+        nc.vector.tensor_scalar(h[1][:], accs[1][:], 0.0625, None, ALU.mult)
+        fetch1(0)
+        fetch1(1)
+        put1([0, 1])
 
         bytes1 = sbuf("bytes1", [P, CODED * PIECE], U8, "bytes")
-        gather_codes(bytes1[:], d_bytes, 1)
+        gather_codes(bytes1[:], d_bytes, 1, l_k)
         move_rows(moved1, bytes1, (nc.sync,))
-        dg1 = sbuf("dg1", [P, CODED * PIECE], U32, "pair0")
-        gather_codes(dg1[:], dw, 1)
-        codes1 = sbuf("codes1", [P, CT], U32)
-        deal_low(codes1[:], dg1[:])
-        plane1 = sbuf("plane1", [P, CT], U8)
-        deal_low(plane1[:], moved1[:])
-        acc1 = product_h("acc1", codes1[:], plane1[:])
-        nc.vector.tensor_scalar(h[1][:], acc1[:], 0.0625, None, ALU.mult)
-        fetch1(1, "pair1")
-        codes23 = sbuf("codes23", [P, 2 * CT], U32, "codes1")
-        plane23 = sbuf("plane23", [P, 2 * CT], U8, "plane1")
-        deal_high(codes23[:], dg0[:], 0)
-        deal_high(codes23[:], dg1[:], 1)
-        deal_high(plane23[:], moved0[:, XS:], 0)
-        deal_high(plane23[:], moved1[:], 1)
-        for x in (2, 3):
-            cols = slice((x - 2) * CT, (x - 1) * CT)
-            acc = product_h("acc%d" % x, codes23[:, cols], plane23[:, cols])
-            nc.vector.tensor_scalar(h[x][:], acc[:], 0.0625, None, ALU.mult)
-        put1(1)
-        fetch1(2, "res1")
-        send1(1)
+        dg1 = sbuf("dg1", [P, CODED * PIECE], U32, "pair1")
+        gather_codes(dg1[:], dw, 1, l_k)
+        accs = product_h(1, dg1[:], moved1[:])
+        for u in range(2):
+            nc.vector.tensor_scalar(h[2 + u][:], accs[u][:], 0.0625, None, ALU.mult)
+        fetch1(2)
+        fetch1(3)
+        put1([2, 3])
 
-        slot0 = sbuf("slot0", [P, S], F32)
-        slot1 = sbuf("slot1", [P, S], F32)
-        low1 = sbuf("low1", [P, S], F32)
+        loss = sbuf("loss", [P, PACK], F32)
+        nc.gpsimd.tensor_scalar(loss[:], gain[:], -1.0, None, ALU.mult)
+        zt = sbuf("zt", [P, PACK, S], BF16)
         zi = sbuf("zi", [P, S, PACK], BF16)
-        nc.vector.tensor_tensor(slot0[:], ub[0][:], ds[0][:, :S], ALU.subtract)
-        nc.sync.dma_start(slot1[:HALF, :], slot0[HALF:, :])
 
-        duob = sbuf("duob", [P, S], U8, "res1")
+        def make_z(x, z, queues):
+            scaled = sbuf("scaled%d" % x, [P, S], F32)
+            nc.vector.tensor_scalar(scaled[:], ub[x][:], gain[:, x : x + 1], None, ALU.mult)
+            nc.vector.scalar_tensor_tensor(z, ds[x][:, :S], loss[:, x : x + 1], scaled[:], ALU.mult, ALU.add)
+            for t in range(PACK):
+                queues[t % len(queues)].dma_start(zt[32 * x : 32 * x + 32, t, :], z[t:P:PACK, :])
+
+        def weave(rows):
+            nc.vector.tensor_copy(
+                zi[rows, :, :].rearrange("p (c i) t -> p c t i", i=4), zt[rows, :, :].rearrange("p t (c i) -> p c t i", i=4)
+            )
+
+        z01 = sbuf("z01", [P, 2 * S], BF16, "pair1")
+        make_z(0, z01[:, :S], (nc.sync,))
+        make_z(1, z01[:, S:], (nc.sync,))
+
+        duob = sbuf("duob", [P, S], U8, "h1")
         gather_tokens(duob[:], x_bytes, [l_duo])
         move_rows(duop, duob, (nc.sync,))
         duog = sbuf("duog", [P, S], U32, "h2")
@@ -212,24 +202,12 @@ def tile_picked_mtthzntcpsdpolar_none_p_kernel(
                 start=True,
                 stop=False,
             )
-        loss = sbuf("loss", [P, PACK], F32)
-        nc.gpsimd.tensor_scalar(loss[:], gain[:], -1.0, None, ALU.mult)
-
-        put1(2)
-        fetch1(3, "res2")
-        send1(2)
-        nc.vector.tensor_tensor(low1[:HALF, :], ub[1][:HALF, :], ds[1][:HALF, :S], ALU.subtract)
-        nc.sync.dma_start(slot0[HALF:, :], low1[:HALF, :])
-        nc.vector.tensor_tensor(slot1[HALF:, :], ub[1][HALF:, :], ds[1][HALF:, :S], ALU.subtract)
-        put1(3)
-        send1(3)
-        nc.vector.tensor_scalar(zi[:, :, 0], slot0[:], gain[:, 0:1], None, ALU.mult)
-        nc.vector.tensor_scalar(zi[:, :, 1], slot1[:], gain[:, 1:2], None, ALU.mult)
-        for x in (2, 3):
-            scaled = sbuf("scaled%d" % x, [P, S], F32)
-            nc.vector.tensor_scalar(scaled[:], ub[x][:], gain[:, x : x + 1], None, ALU.mult)
-            nc.vector.scalar_tensor_tensor(zi[:, :, x], ds[x][:, :S], loss[:, x : x + 1], scaled[:], ALU.mult, ALU.add)
-
+        weave(slice(0, HALF))
+        z2 = sbuf("z2", [P, S], BF16)
+        make_z(2, z2[:], (nc.sync,))
+        z3 = sbuf("z3", [P, S], BF16)
+        make_z(3, z3[:], (nc.sync, nc.scalar))
+        weave(slice(HALF, P))
         zq = sbuf("zq", [P, S], U32)
         zs = sbuf("zs", [P, S], U8)
         nc.vector.quantize_mx(out=zq[:].bitcast(FP8X4), scales=zs[:], in_=zi[:].rearrange("p c t -> p (c t)"))

@@ -73,8 +73,7 @@ def tile_picked_mtthzntcpsdpolar_none_p_kernel(
         w2w = load_words("w2w", w2_words, nc.sync)
         w1w = load_words("w1w", w1_words, nc.sync)
         gain = sbuf("gain", [P, PACK], F32)
-        with nc.allow_non_contiguous_dma(reason="one gain a row"):
-            nc.gpsimd.dma_start(gain[:], gn.rearrange("(t p) o -> p (t o)", p=P))
+        nc.gpsimd.dma_start(gain[:], gn.rearrange("(p t) o -> p (t o)", t=PACK))
         for j, src in enumerate((w1_scales, w2_scales)):
             for q in range(4):
                 nc.gpsimd.dma_start(
@@ -114,11 +113,10 @@ def tile_picked_mtthzntcpsdpolar_none_p_kernel(
             accs = [psum.tile([P, S], F32, name="acc%d" % (2 * piece + u)) for u in range(2)]
             for j in range(CODED):
                 for u in range(2):
-                    cols = slice(j * PIECE + u * P, j * PIECE + (u + 1) * P)
                     nc.tensor.matmul_mx(
                         out=accs[u][:],
-                        lhsT=codes[:, cols].bitcast(FP8X4),
-                        lhsT_scale=plane[:, cols],
+                        lhsT=codes[j][:, u * P : (u + 1) * P].bitcast(FP8X4),
+                        lhsT_scale=plane[:, j * PIECE + u * P : j * PIECE + (u + 1) * P],
                         rhs=xg[:, j * S : (j + 1) * S].bitcast(FP8X4),
                         rhs_scale=moved0[:, j * S : (j + 1) * S],
                         start=(j == 0),
@@ -128,68 +126,56 @@ def tile_picked_mtthzntcpsdpolar_none_p_kernel(
 
         h = [sbuf("h%d" % x, [P, S], F32) for x in range(4)]
         ub = [sbuf("ub%d" % x, [P, S], F32) for x in range(4)]
-        ds = [sbuf("ds%d" % x, [P, 2 * S], F32) for x in range(4)]
-        res = [sbuf("res%d" % x, [P, S], F32) for x in range(4)]
+        uy = [sbuf("uy%d" % y, [P, S], F32) for y in range(4)]
+        least = [sbuf("least%d" % x, [P, W], F32) for x in range(4)]
+        total = [sbuf("total%d" % piece, [P, 2, W], F32) for piece in range(2)]
 
-        def fetch1(x):
-            pair = sbuf("pair%d" % x, [P, S], F32)
-            nc.scalar.activation(pair[:, :W], h[x][:].indirect(l_n1[:]), ACT.Copy)
-            nc.scalar.activation(pair[:, W:], h[x][:].indirect(l_n2[:]), ACT.Copy)
-            nc.vector.tensor_tensor(res[x][:, :W], pair[:, :W], pair[:, W:], ALU.min)
-            nc.vector.tensor_tensor(res[x][:, W:], pair[:, :W], pair[:, W:], ALU.add)
+        def fetch1(piece):
+            pair = sbuf("pair%d" % piece, [P, 2, S], F32)
+            for u in range(2):
+                x = 2 * piece + u
+                nc.scalar.activation(pair[:, u, :W], h[x][:].indirect(l_n1[:]), ACT.Copy)
+                nc.scalar.activation(pair[:, u, W:], h[x][:].indirect(l_n2[:]), ACT.Copy)
+                nc.vector.tensor_tensor(least[x][:], pair[:, u, :W], pair[:, u, W:], ALU.min)
+            nc.vector.tensor_tensor(total[piece][:], pair[:, :, :W], pair[:, :, W:], ALU.add)
 
-        def put1(xs):
+        def put1(piece):
+            xs = (2 * piece, 2 * piece + 1)
             for x in xs:
-                nc.scalar.activation(ub[x][:].indirect(l_n3[:]), res[x][:, :W], ACT.Copy)
+                nc.scalar.activation(ub[x][:].indirect(l_n3[:]), least[x][:], ACT.Copy)
             for x in xs:
-                nc.scalar.activation(ub[x][:].indirect(l_n4[:]), res[x][:, W:], ACT.Copy)
+                nc.scalar.activation(ub[x][:].indirect(l_n4[:]), total[piece][:, x % 2, :], ACT.Copy)
             for x in xs:
-                nc.scalar.activation(ds[x][:].indirect(l_n5[:]), ub[x][:], ACT.Copy)
+                for t in range(PACK):
+                    y, first = (x // 2, HALF * t + 32 * (x % 2)) if t < 2 else (t, 32 * x)
+                    nc.sync.dma_start(uy[y][first : first + 32, :], ub[x][t:P:PACK, :])
 
-        accs = product_h(0, dg0[:], moved0[:, XS:])
-        nc.scalar.activation(h[0][:], accs[0][:], ACT.Copy, scale=0.0625)
-        nc.vector.tensor_scalar(h[1][:], accs[1][:], 0.0625, None, ALU.mult)
-        fetch1(0)
-        fetch1(1)
-        put1([0, 1])
-
+        accs = product_h(0, [dg0[:, j * PIECE : (j + 1) * PIECE] for j in range(CODED)], moved0[:, XS:])
         bytes1 = sbuf("bytes1", [P, CODED * PIECE], U8, "bytes")
         gather_codes(bytes1[:], d_bytes, 1, l_k)
         move_rows(moved1, bytes1, (nc.sync,))
-        dg1 = sbuf("dg1", [P, CODED * PIECE], U32, "pair1")
-        gather_codes(dg1[:], dw, 1, l_k)
-        accs = product_h(1, dg1[:], moved1[:])
+        nc.scalar.activation(h[0][:], accs[0][:], ACT.Copy, scale=0.0625)
+        nc.vector.tensor_scalar(h[1][:], accs[1][:], 0.0625, None, ALU.mult)
+        dg1a = sbuf("dg1a", [P, PIECE], U32, "dg0")
+        gather_codes(dg1a[:], dw, 1, l_k[:1])
+        fetch1(0)
+        put1(0)
+
+        dg1b = sbuf("dg1b", [P, 2 * PIECE], U32, "pair0")
+        gather_codes(dg1b[:], dw, 1, l_k[1:])
+        accs = product_h(1, [dg1a[:], dg1b[:, :PIECE], dg1b[:, PIECE:]], moved1[:])
         for u in range(2):
             nc.vector.tensor_scalar(h[2 + u][:], accs[u][:], 0.0625, None, ALU.mult)
-        fetch1(2)
-        fetch1(3)
-        put1([2, 3])
+        fetch1(1)
+        put1(1)
 
-        loss = sbuf("loss", [P, PACK], F32)
-        nc.gpsimd.tensor_scalar(loss[:], gain[:], -1.0, None, ALU.mult)
-        zt = sbuf("zt", [P, PACK, S], BF16)
-        zi = sbuf("zi", [P, S, PACK], BF16)
-
-        def make_z(x, z, queues):
-            scaled = sbuf("scaled%d" % x, [P, S], F32)
-            nc.vector.tensor_scalar(scaled[:], ub[x][:], gain[:, x : x + 1], None, ALU.mult)
-            nc.vector.scalar_tensor_tensor(z, ds[x][:, :S], loss[:, x : x + 1], scaled[:], ALU.mult, ALU.add)
-            for t in range(PACK):
-                queues[t % len(queues)].dma_start(zt[32 * x : 32 * x + 32, t, :], z[t:P:PACK, :])
-
-        def weave(rows):
-            nc.vector.tensor_copy(
-                zi[rows, :, :].rearrange("p (c i) t -> p c t i", i=4), zt[rows, :, :].rearrange("p t (c i) -> p c t i", i=4)
-            )
-
-        z01 = sbuf("z01", [P, 2 * S], BF16, "pair1")
-        make_z(0, z01[:, :S], (nc.sync,))
-        make_z(1, z01[:, S:], (nc.sync,))
-
-        duob = sbuf("duob", [P, S], U8, "h1")
+        duob = sbuf("duob", [P, S], U8, "h3")
         gather_tokens(duob[:], x_bytes, [l_duo])
         move_rows(duop, duob, (nc.sync,))
-        duog = sbuf("duog", [P, S], U32, "h2")
+        loss = sbuf("loss", [P, PACK], F32)
+        nc.gpsimd.tensor_scalar(loss[:], gain[:], -1.0, None, ALU.mult)
+
+        duog = sbuf("duog", [P, S], U32, "pair1")
         gather_tokens(duog[:], xw, [l_duo])
         acc2 = [psum.tile([P, S], F32, name="out_acc%d" % t) for t in range(4)]
         for t in range(4):
@@ -202,12 +188,26 @@ def tile_picked_mtthzntcpsdpolar_none_p_kernel(
                 start=True,
                 stop=False,
             )
-        weave(slice(0, HALF))
-        z2 = sbuf("z2", [P, S], BF16)
-        make_z(2, z2[:], (nc.sync,))
-        z3 = sbuf("z3", [P, S], BF16)
-        make_z(3, z3[:], (nc.sync, nc.scalar))
-        weave(slice(HALF, P))
+
+        ds = [sbuf("ds%d" % y, [P, 2 * S], F32, "total1" if y == 0 else None) for y in range(4)]
+        for y in range(4):
+            nc.scalar.activation(ds[y][:].indirect(l_n5[:]), uy[y][:], ACT.Copy)
+        slot0 = sbuf("slot0", [P, S], F32)
+        slot1 = sbuf("slot1", [P, S], F32)
+        low1 = sbuf("low1", [P, S], F32)
+        zi = sbuf("zi", [P, S, PACK], BF16)
+        nc.vector.tensor_tensor(slot0[:], uy[0][:], ds[0][:, :S], ALU.subtract)
+        nc.sync.dma_start(slot1[:HALF, :], slot0[HALF:, :])
+        nc.vector.tensor_tensor(low1[:HALF, :], uy[1][:HALF, :], ds[1][:HALF, :S], ALU.subtract)
+        nc.sync.dma_start(slot0[HALF:, :], low1[:HALF, :])
+        nc.vector.tensor_tensor(slot1[HALF:, :], uy[1][HALF:, :], ds[1][HALF:, :S], ALU.subtract)
+        scaled = [sbuf("scaled%d" % y, [P, S], F32) for y in range(2)]
+        for y in range(2):
+            nc.vector.tensor_scalar(scaled[y][:], uy[2 + y][:], gain[:, 2 + y : 3 + y], None, ALU.mult)
+        nc.vector.tensor_scalar(zi[:, :, 1], slot1[:], gain[:, 1:2], None, ALU.mult)
+        nc.vector.scalar_tensor_tensor(zi[:, :, 2], ds[2][:, :S], loss[:, 2:3], scaled[0][:], ALU.mult, ALU.add)
+        nc.vector.tensor_scalar(zi[:, :, 0], slot0[:], gain[:, 0:1], None, ALU.mult)
+        nc.vector.scalar_tensor_tensor(zi[:, :, 3], ds[3][:, :S], loss[:, 3:4], scaled[1][:], ALU.mult, ALU.add)
         zq = sbuf("zq", [P, S], U32)
         zs = sbuf("zs", [P, S], U8)
         nc.vector.quantize_mx(out=zq[:].bitcast(FP8X4), scales=zs[:], in_=zi[:].rearrange("p c t -> p (c t)"))

@@ -54,6 +54,10 @@ def tile_picked_mtthzntcpsdpolar_none_p_kernel(
             nc.vector.memset(plane[:].bitcast(I32), 0)
         for plane in (x_bytes, moved1, duop, w_bytes):
             nc.gpsimd.memset(plane[:].bitcast(I32), 0)
+        warm_in = sbuf("warm_in", [P, 1], F32)
+        warm_out = sbuf("warm_out", [P, 1], F32)
+        nc.gpsimd.memset(warm_in[:], 1.0)
+        nc.scalar.activation(warm_out[:], warm_in[:], ACT.Sqrt)
         nc.sync.dma_start(x_bytes[0:P:8, :].bitcast(I32), x_scales[0].bitcast(I32))
         nc.sync.dma_start(d_bytes[0:P:8, :].bitcast(I32), d_scales[0].bitcast(I32))
         l_offs = load_list("l_offs", offs)

from contextlib import ExitStack

import concourse.mybir as mybir

K, T, S, N, G, H, W = 512, 1024, 256, 512, 2048, 512, 128
FLOPS = 2 * K * S * (3 * H + 2 * N)

F32 = mybir.dt.float32
BF16 = mybir.dt.bfloat16
I32 = mybir.dt.int32
U32 = mybir.dt.uint32
U16 = mybir.dt.uint16
U8 = mybir.dt.uint8
FP8X4 = mybir.dt.float8_e4m3fn_x4
ALU = mybir.AluOpType
ACT = mybir.ActivationFunctionType

P = 128
HALF = P // 2
PACK = 4
CODED = 3
PIECE = H // 2


def tile_picked_mtthzntcpsdpolar_none_p_kernel(
    tc, x_words, x_scales, d_words, d_scales, gn, w1_words, w1_scales, w2_words, w2_scales,
    offs, k1, two, k2, hz, k3, n1, n2, n3, n4, n5, duo, n6, n7, out,
):
    nc = tc.nc
    with ExitStack() as ctx:
        held = ctx.enter_context(tc.tile_pool(name="held", bufs=1))
        psum = ctx.enter_context(tc.psum_pool(name="psum", bufs=1))

        def sbuf(name, shape, dtype, tag=None):
            return held.tile(shape, dtype, name=name, tag=tag or name, align_bytes=64)

        def load_list(name, src):
            lst = held.tile(list(src.shape), U16, name=name)
            nc.sync.dma_start(lst[:], src)
            return lst

        def load_words(name, src, queue):
            words = sbuf(name, [P, src.shape[2]], U32)
            queue.dma_start(words[:].bitcast(I32), src[0].rearrange("p n t -> p (n t)").bitcast(I32))
            return words

        x_bytes = sbuf("x_bytes", [P, T], U8)
        d_bytes = sbuf("d_bytes", [P, G], U8)
        w_bytes = sbuf("w_bytes", [P, 2 * N], U8)
        moved0 = sbuf("moved0", [P, CODED * (S + PIECE)], U8)
        moved1 = sbuf("moved1", [P, CODED * PIECE], U8)
        duop = sbuf("duop", [P, S], U8)
        for plane in (d_bytes, moved0):
            nc.vector.memset(plane[:].bitcast(I32), 0)
        for plane in (x_bytes, moved1, duop, w_bytes):
            nc.gpsimd.memset(plane[:].bitcast(I32), 0)
        warm_in = sbuf("warm_in", [P, 1], F32)
        warm_out = sbuf("warm_out", [P, 1], F32)
        nc.gpsimd.memset(warm_in[:], 1.0)
        nc.scalar.activation(warm_out[:], warm_in[:], ACT.Sqrt)
        nc.sync.dma_start(x_bytes[0:P:8, :].bitcast(I32), x_scales[0].bitcast(I32))
        nc.sync.dma_start(d_bytes[0:P:8, :].bitcast(I32), d_scales[0].bitcast(I32))
        l_offs = load_list("l_offs", offs)
        l_two = load_list("l_two", two)
        l_hz = load_list("l_hz", hz)
        l_k = [load_list("l_k1", k1), load_list("l_k2", k2), load_list("l_k3", k3)]
        xw = load_words("xw", x_words, nc.sync)
        dw = load_words("dw", d_words, nc.sync)
        l_n1 = load_list("l_n1", n1)
        l_n2 = load_list("l_n2", n2)
        l_n3 = load_list("l_n3", n3)
        l_n4 = load_list("l_n4", n4)
        l_n5 = load_list("l_n5", n5)
        l_duo = load_list("l_duo", duo)
        l_n6 = load_list("l_n6", n6)
        l_n7 = load_list("l_n7", n7)
        w2w = load_words("w2w", w2_words, nc.sync)
        w1w = load_words("w1w", w1_words, nc.sync)
        gain = sbuf("gain", [P, PACK], F32)
        nc.gpsimd.dma_start(gain[:], gn.rearrange("(p t) o -> p (t o)", t=PACK))
        for j, src in enumerate((w1_scales, w2_scales)):
            for q in range(4):
                nc.gpsimd.dma_start(
                    w_bytes[32 * q : 32 * q + 4, j * N : (j + 1) * N].bitcast(I32),
                    src[0][4 * q : 4 * q + 4, :].bitcast(I32),
                )
        l_x = [l_offs, l_two, l_hz]

        def gather_tokens(got, table, lists):
            for j, lst in enumerate(lists):
                nc.vector.tensor_copy(got[:, j * S : (j + 1) * S], table[:].indirect(lst[:]))

        def gather_codes(got, table, piece, lists):
            cols = slice(piece * PIECE // 16, (piece + 1) * PIECE // 16)
            for j, lst in enumerate(lists):
                nc.vector.tensor_copy(got[:, j * PIECE : (j + 1) * PIECE], table[:].indirect(lst[:, cols]))

        def move_rows(dst, src, queues):
            for q in range(4):
                queues[q % len(queues)].dma_start(
                    dst[32 * q : 32 * q + 4, :].bitcast(I32), src[32 * q : 32 * q + 32 : 8, :].bitcast(I32)
                )

        XS = CODED * S
        CT = CODED * P

        bytes0 = sbuf("bytes0", [P, XS + CODED * PIECE], U8, "bytes")
        gather_tokens(bytes0[:, :XS], x_bytes, l_x)
        gather_codes(bytes0[:, XS:], d_bytes, 0, l_k)
        move_rows(moved0, bytes0, (nc.scalar,))
        xg = sbuf("xg", [P, XS], U32)
        gather_tokens(xg[:], xw, l_x)
        dg0 = sbuf("dg0", [P, CODED * PIECE], U32)
        gather_codes(dg0[:], dw, 0, l_k)

        def product_h(piece, codes, plane):
            accs = [psum.tile([P, S], F32, name="acc%d" % (2 * piece + u)) for u in range(2)]
            for j in range(CODED):
                for u in range(2):
                    nc.tensor.matmul_mx(
                        out=accs[u][:],
                        lhsT=codes[j][:, u * P : (u + 1) * P].bitcast(FP8X4),
                        lhsT_scale=plane[:, j * PIECE + u * P : j * PIECE + (u + 1) * P],
                        rhs=xg[:, j * S : (j + 1) * S].bitcast(FP8X4),
                        rhs_scale=moved0[:, j * S : (j + 1) * S],
                        start=(j == 0),
                        stop=(j == CODED - 1),
                    )
            return accs

        h = [sbuf("h%d" % x, [P, S], F32) for x in range(4)]
        ub = [sbuf("ub%d" % x, [P, S], F32) for x in range(4)]
        uy = [sbuf("uy%d" % y, [P, S], F32) for y in range(4)]
        least = [sbuf("least%d" % x, [P, W], F32) for x in range(4)]
        total = [sbuf("total%d" % piece, [P, 2, W], F32) for piece in range(2)]

        def fetch1(piece):
            pair = sbuf("pair%d" % piece, [P, 2, S], F32)
            for u in range(2):
                x = 2 * piece + u
                nc.scalar.activation(pair[:, u, :W], h[x][:].indirect(l_n1[:]), ACT.Copy)
                nc.scalar.activation(pair[:, u, W:], h[x][:].indirect(l_n2[:]), ACT.Copy)
                nc.vector.tensor_tensor(least[x][:], pair[:, u, :W], pair[:, u, W:], ALU.min)
            nc.vector.tensor_tensor(total[piece][:], pair[:, :, :W], pair[:, :, W:], ALU.add)

        def put1(piece):
            xs = (2 * piece, 2 * piece + 1)
            for x in xs:
                nc.scalar.activation(ub[x][:].indirect(l_n3[:]), least[x][:], ACT.Copy)
            for x in xs:
                nc.scalar.activation(ub[x][:].indirect(l_n4[:]), total[piece][:, x % 2, :], ACT.Copy)
            for x in xs:
                for t in range(PACK):
                    y, first = (x // 2, HALF * t + 32 * (x % 2)) if t < 2 else (t, 32 * x)
                    nc.sync.dma_start(uy[y][first : first + 32, :], ub[x][t:P:PACK, :])

        accs = product_h(0, [dg0[:, j * PIECE : (j + 1) * PIECE] for j in range(CODED)], moved0[:, XS:])
        bytes1 = sbuf("bytes1", [P, CODED * PIECE], U8, "bytes")
        gather_codes(bytes1[:], d_bytes, 1, l_k)
        move_rows(moved1, bytes1, (nc.sync,))
        nc.scalar.activation(h[0][:], accs[0][:], ACT.Copy, scale=0.0625)
        nc.vector.tensor_scalar(h[1][:], accs[1][:], 0.0625, None, ALU.mult)
        dg1a = sbuf("dg1a", [P, PIECE], U32, "dg0")
        gather_codes(dg1a[:], dw, 1, l_k[:1])
        fetch1(0)
        put1(0)

        dg1b = sbuf("dg1b", [P, 2 * PIECE], U32, "pair0")
        gather_codes(dg1b[:], dw, 1, l_k[1:])
        accs = product_h(1, [dg1a[:], dg1b[:, :PIECE], dg1b[:, PIECE:]], moved1[:])
        for u in range(2):
            nc.vector.tensor_scalar(h[2 + u][:], accs[u][:], 0.0625, None, ALU.mult)
        fetch1(1)
        put1(1)

        duob = sbuf("duob", [P, S], U8, "h3")
        gather_tokens(duob[:], x_bytes, [l_duo])
        move_rows(duop, duob, (nc.sync,))
        loss = sbuf("loss", [P, PACK], F32)
        nc.gpsimd.tensor_scalar(loss[:], gain[:], -1.0, None, ALU.mult)

        duog = sbuf("duog", [P, S], U32, "pair1")
        gather_tokens(duog[:], xw, [l_duo])
        acc2 = [psum.tile([P, S], F32, name="out_acc%d" % t) for t in range(4)]
        for t in range(4):
            nc.tensor.matmul_mx(
                out=acc2[t][:],
                lhsT=w2w[:, t * P : (t + 1) * P].bitcast(FP8X4),
                lhsT_scale=w_bytes[:, N + t * P : N + (t + 1) * P],
                rhs=duog[:].bitcast(FP8X4),
                rhs_scale=duop[:],
                start=True,
                stop=False,
            )

        ds = [sbuf("ds%d" % y, [P, 2 * S], F32, "total1" if y == 0 else None) for y in range(4)]
        for y in range(4):
            nc.scalar.activation(ds[y][:].indirect(l_n5[:]), uy[y][:], ACT.Copy)
        slot0 = sbuf("slot0", [P, S], F32)
        slot1 = sbuf("slot1", [P, S], F32)
        low1 = sbuf("low1", [P, S], F32)
        zi = sbuf("zi", [P, S, PACK], BF16)
        nc.vector.tensor_tensor(slot0[:], uy[0][:], ds[0][:, :S], ALU.subtract)
        nc.sync.dma_start(slot1[:HALF, :], slot0[HALF:, :])
        nc.vector.tensor_tensor(low1[:HALF, :], uy[1][:HALF, :], ds[1][:HALF, :S], ALU.subtract)
        nc.sync.dma_start(slot0[HALF:, :], low1[:HALF, :])
        nc.vector.tensor_tensor(slot1[HALF:, :], uy[1][HALF:, :], ds[1][HALF:, :S], ALU.subtract)
        scaled = [sbuf("scaled%d" % y, [P, S], F32) for y in range(2)]
        for y in range(2):
            nc.vector.tensor_scalar(scaled[y][:], uy[2 + y][:], gain[:, 2 + y : 3 + y], None, ALU.mult)
        nc.vector.tensor_scalar(zi[:, :, 1], slot1[:], gain[:, 1:2], None, ALU.mult)
        nc.vector.scalar_tensor_tensor(zi[:, :, 2], ds[2][:, :S], loss[:, 2:3], scaled[0][:], ALU.mult, ALU.add)
        nc.vector.tensor_scalar(zi[:, :, 0], slot0[:], gain[:, 0:1], None, ALU.mult)
        nc.vector.scalar_tensor_tensor(zi[:, :, 3], ds[3][:, :S], loss[:, 3:4], scaled[1][:], ALU.mult, ALU.add)
        zq = sbuf("zq", [P, S], U32)
        zs = sbuf("zs", [P, S], U8)
        nc.vector.quantize_mx(out=zq[:].bitcast(FP8X4), scales=zs[:], in_=zi[:].rearrange("p c t -> p (c t)"))
        for t in range(4):
            nc.tensor.matmul_mx(
                out=acc2[t][:],
                lhsT=w1w[:, t * P : (t + 1) * P].bitcast(FP8X4),
                lhsT_scale=w_bytes[:, t * P : (t + 1) * P],
                rhs=zq[:].bitcast(FP8X4),
                rhs_scale=zs[:],
                start=False,
                stop=True,
            )

        h2 = [sbuf("g%d" % t, [P, S], F32) for t in range(4)]
        pair2 = [sbuf("pairb%d" % t, [P, S], F32) for t in range(4)]
        square = [sbuf("square%d" % t, [P, S], F32) for t in range(4)]
        diff2 = [sbuf("diffb%d" % t, [P, W], F32) for t in range(4)]
        radic = [sbuf("radic%d" % t, [P, W], F32) for t in range(4)]
        root = [sbuf("root%d" % t, [P, W], F32) for t in range(4)]
        done = [sbuf("done%d" % t, [P, S], F32) for t in range(4)]

        def fetch2(t):
            nc.scalar.activation(pair2[t][:, :W], h2[t][:].indirect(l_n6[:]), ACT.Copy)
            nc.scalar.activation(pair2[t][:, W:], h2[t][:].indirect(l_n7[:]), ACT.Copy)
            nc.vector.scalar_tensor_tensor(diff2[t][:], pair2[t][:, :W], -0.5, pair2[t][:, W:], ALU.mult, ALU.add)
            nc.vector.tensor_tensor(square[t][:], pair2[t][:], pair2[t][:], ALU.mult)
            nc.vector.scalar_tensor_tensor(radic[t][:], square[t][:, :W], 0.25, square[t][:, W:], ALU.add, ALU.add)

        def put2(t):
            nc.scalar.activation(done[t][:].indirect(l_n7[:]), diff2[t][:], ACT.Copy)
            nc.scalar.activation(root[t][:], radic[t][:], ACT.Sqrt)
            nc.scalar.activation(done[t][:].indirect(l_n6[:]), root[t][:], ACT.Copy)
            nc.sync.dma_start(out[t * P : (t + 1) * P, :], done[t][:])

        nc.scalar.activation(h2[0][:], acc2[0][:], ACT.Copy)
        for t in range(1, 4):
            nc.vector.tensor_copy(h2[t][:], acc2[t][:])
        fetch2(0)
        for t in range(4):
            if t + 1 < 4:
                fetch2(t + 1)
            put2(t)
